import numpy as np
import ml_dtypes


def mxq(x, axis, fmt="e4m3"):
    dtype, down = {"e4m3": (ml_dtypes.float8_e4m3fn, 7), "e5m2": (ml_dtypes.float8_e5m2, 14)}[fmt]
    v = np.moveaxis(np.asarray(x, np.float32).astype(ml_dtypes.bfloat16).astype(np.float64), axis, -1)
    blocks = v.reshape(v.shape[:-1] + (-1, 32))
    amax = np.abs(blocks).max(-1, keepdims=True)
    byte = np.maximum(np.where(amax > 0, np.frexp(amax)[1] - 1 + 127, 0) - down, 1)
    scale = np.exp2(byte - 127.0)
    codes = (blocks / scale).astype(np.float32).astype(dtype).astype(np.float64)
    return np.moveaxis((codes * scale).reshape(v.shape), -1, axis)


WIDE = False


def mx_kscale(k):
    if not WIDE:
        return np.ones(k)
    levels = np.array([10, -10, 5, -5, 0])
    if k % 512:
        return np.exp2(np.random.permutation(np.resize(levels, k // 32))).repeat(32)
    a = np.empty((k // 512, 16))
    for p in range(k // 512):
        a[p, :8] = np.random.permutation(np.resize(levels, 8))
        for g in range(8):
            far = levels[np.abs(levels - a[p, g]) >= 10]
            a[p, g + 8] = far[np.random.randint(len(far))]
    return np.exp2(a.ravel()).repeat(32)


def f64(x):
    return np.asarray(x).astype(np.float64)


def striped(idx):
    return np.tile(idx.reshape(-1, 16).T, (8, 1)).astype(np.uint16)


def unstriped(offs):
    return offs[:16].T.reshape(-1).astype(np.int64)


def striped8(idx):
    return np.concatenate([x.reshape(-1, 16).T for x in idx]).astype(np.uint16)


def runs(offs, k):
    lists = np.stack([offs[16 * r : 16 * r + 16].T.reshape(-1) for r in range(8)]).astype(np.int64)
    return lists[np.arange(k) % 512 // 64]


def pack_weight(w):
    k, n = w.shape
    w = f64(np.asarray(w, np.float32).astype(ml_dtypes.bfloat16)).reshape(k // 32, 32, n)
    amax = np.abs(w).max(1)
    byte = np.clip(np.where(amax > 0, np.frexp(amax)[1] - 1 + 127 - 7, 1), 1, 254)
    scaled = (w * np.exp2(127.0 - byte)[:, None, :]).reshape(k, n).astype(np.float32)
    words = np.ascontiguousarray(scaled.reshape(k // 512, 128, 4, n).transpose(0, 1, 3, 2)).astype(ml_dtypes.float8_e4m3fn).view(np.uint8)
    return words, np.ascontiguousarray(byte.astype(np.uint8).reshape(k // 512, 16, n))


def unpack_weight(words, scales):
    g, p, n, _ = words.shape
    vals = np.ascontiguousarray(words).view(ml_dtypes.float8_e4m3fn).astype(np.float64) * np.repeat(np.exp2(scales.astype(np.float64) - 127.0), 8, axis=1)[..., None]
    return vals.transpose(0, 1, 3, 2).reshape(g * 512, n)

def planes(y):
    n, m = y.shape
    v = y.astype(np.float32).astype(ml_dtypes.bfloat16).astype(np.float64).reshape(n // 32, 32, m)
    top = np.abs(v).max(1)
    byte = np.clip(np.where(top > 0, np.frexp(top)[1] - 1 + 127 - 7, 1), 1, 254)
    codes = (v * np.exp2(127.0 - byte)[:, None, :]).reshape(n, m).astype(np.float32).astype(ml_dtypes.float8_e4m3fn).view(np.uint8)
    words = codes.reshape(n // 512, 128, 4, m).transpose(0, 1, 3, 2)
    return np.ascontiguousarray(words), np.ascontiguousarray(byte.astype(np.uint8).reshape(n // 512, 16, m))


K, T, S, N, H = 512, 2048, 512, 512, 512


def setup_inputs():
    n = np.random.standard_normal
    s = mx_kscale(K)[:, None]
    u = mx_kscale(S)
    packed_xT = pack_weight(n((K, T)) * s)
    return {
        "x_words": packed_xT[0],
        "x_scales": packed_xT[1],
        "wa": (n((K, H)) / np.sqrt(K) / s).astype(np.float32),
        "wb": (n((K, N)) / np.sqrt(K) / s).astype(np.float32),
        "gt": (np.random.uniform(0.5, 1.5, (S, 1)) * u[:, None]).astype(np.float32),
        "gi": (np.random.uniform(0.5, 1.5, (S, 1)) / u[:, None]).astype(np.float32),
        "offs": striped(np.random.permutation(T)[:S]),
        "two": striped(np.random.permutation(T)[:S]),
        "n1": striped(np.random.permutation(H)),
        "n2": striped(np.random.permutation(H)),
        "n3": striped8(np.stack([np.random.permutation(N) for _ in range(8)])),
    }


def reference(x_words, x_scales, wa, wb, gt, gi, offs, two, n1, n2, n3):
    xq = unpack_weight(x_words, x_scales)[:, unstriped(offs)]
    a = xq.T @ mxq(f64(wa), 0, "e4m3")
    pa = a[:, unstriped(n1)]
    kr = np.exp(-0.5 * ((a - pa) ** 2))
    pb = a[:, unstriped(n2)]
    kr2 = np.exp(-0.5 * ((a - pb) ** 2))
    z = f64(gt) * ((kr * pa + kr2 * pb) / (kr + kr2 + 0.5))
    x_two = unpack_weight(x_words, x_scales)[:, unstriped(two)]
    b = x_two.T @ mxq(f64(wb), 0, "e4m3")
    z2 = f64(gi) * b
    cv = 0.0625 * ((mxq(z, 0, "e4m3").T @ mxq(z2, 0, "e4m3")))
    out_0 = np.maximum(cv, cv[np.arange(H)[:, None], runs(n3, H)])
    return (out_0,) + planes(out_0)

from contextlib import ExitStack

import concourse.mybir as mybir

K, T, S, N, H = 512, 2048, 512, 512, 512
FLOPS = 3 * 2 * 512 * 512 * 512

F32 = mybir.dt.float32
BF16 = mybir.dt.bfloat16
I32 = mybir.dt.int32
U32 = mybir.dt.uint32
U16 = mybir.dt.uint16
U8 = mybir.dt.uint8
FP8X4 = mybir.dt.float8_e4m3fn_x4
ACT = mybir.ActivationFunctionType
ALU = mybir.AluOpType

P = 128
PACK = 4
M = 128
HALF = 256


def tile_picked_momkernbig_none_po_kernel(
    tc, x_words, x_scales, wa, wb, gt, gi, offs, two, n1, n2, n3, out_0, out_1, out_2
):
    nc = tc.nc
    with ExitStack() as ctx:
        keep = ctx.enter_context(tc.tile_pool(name="keep", bufs=1))
        ring = ctx.enter_context(tc.tile_pool(name="ring", bufs=3))
        psum = ctx.enter_context(tc.psum_pool(name="psum", bufs=8))

        def load_list(src, name):
            lst = keep.tile([P, S // 16], U16, name=name)
            nc.sync.dma_start(lst[:], src)
            return lst

        def load_weight_half(w, h, name):
            raw = keep.tile([P, PACK, HALF], F32, name=name)
            nc.sync.dma_start(raw[:], w.rearrange("(p j) c -> p j c", j=PACK)[:, :, h * HALF : (h + 1) * HALF])
            return raw

        def load_gate(src, name):
            gate = keep.tile([P, PACK], F32, name=name)
            nc.sync.dma_start(gate[:], src.rearrange("(p t) o -> p (t o)", t=PACK))
            return gate

        xs = keep.tile([P, T], U8, name="xs", align_bytes=64)
        nc.vector.memset(xs[:].bitcast(I32), 0)
        half_c = keep.tile([P, 1], F32, name="half_c")
        nc.vector.memset(half_c[:], 0.5)
        offs_l = load_list(offs, "offs_l")
        two_l = load_list(two, "two_l")
        for q in range(4):
            nc.sync.dma_start(xs[32 * q : 32 * q + 4, :].bitcast(I32), x_scales[0, 4 * q : 4 * q + 4, :].bitcast(I32))
        xw = keep.tile([P, T], U32, name="xw", align_bytes=64)
        nc.sync.dma_start(xw[:].bitcast(I32), x_words[0].rearrange("p n t -> p (n t)").bitcast(I32))
        wa_raw = [load_weight_half(wa, h, "wa_raw%d" % h) for h in range(2)]
        n1_l = load_list(n1, "n1_l")
        n2_l = load_list(n2, "n2_l")
        gt_sb = load_gate(gt, "gt_sb")
        wb_raw = [load_weight_half(wb, h, "wb_raw%d" % h) for h in range(2)]
        gi_sb = load_gate(gi, "gi_sb")
        n3_l = load_list(n3, "n3_l")

        def pick(window, lst, dtype, name, tag):
            picked = keep.tile([P, PACK, M], dtype, name=name, tag=tag, align_bytes=64)
            nc.vector.tensor_copy(picked[:].rearrange("p t m -> p m t"), window[:].indirect(lst[:]))
            return picked

        def interleave(copy, dst, src):
            copy(dst.rearrange("p (c i) t -> p c t i", i=4), src.rearrange("p t (c i) -> p c t i", i=4))

        def quantize_into(codes, scales, grouped):
            nc.vector.quantize_mx(out=codes.bitcast(FP8X4), scales=scales, in_=grouped[:].rearrange("p c t -> p (c t)"))

        def planes(width, name):
            codes = keep.tile([P, width], U32, name=name + "_w", align_bytes=64)
            scales = keep.tile([P, width], U8, name=name + "_s", align_bytes=64)
            return codes, scales

        def quantize(grouped, width, name):
            codes, scales = planes(width, name)
            quantize_into(codes[:], scales[:], grouped)
            return codes, scales

        def product(acc, lhs_w, lhs_s, rhs_w, rhs_s):
            nc.tensor.matmul_mx(out=acc, lhsT=lhs_w.bitcast(FP8X4), lhsT_scale=lhs_s, rhs=rhs_w.bitcast(FP8X4), rhs_scale=rhs_s, start=True, stop=True)

        xa_s = pick(xs, offs_l, U8, "xa_s", "xa_s")
        xb_s = pick(xs, two_l, U8, "xb_s", "xb_s")
        xa_w = pick(xw, offs_l, U32, "xa_w", "xa_w")

        wa_w, wa_s = planes(H, "wa_q")
        for h in range(2):
            cols = slice(h * HALF, (h + 1) * HALF)
            split = (96, 96)[h]
            grouped = keep.tile([P, HALF, PACK], BF16, name="wa_g%d" % h, tag="wa_g%d" % h, align_bytes=64)
            interleave(nc.scalar.copy, grouped[:, :split, :], wa_raw[h][:, :, :split])
            if split < HALF:
                interleave(nc.vector.tensor_copy, grouped[:, split:, :], wa_raw[h][:, :, split:])
            quantize_into(wa_w[:, cols], wa_s[:, cols], grouped)

        a_sb = [keep.tile([P, H], F32, name="a%d" % t) for t in range(PACK)]
        for h in range(2):
            cols = slice(h * HALF, (h + 1) * HALF)
            acc = psum.tile([P, HALF], F32, name="acc")
            product(acc[:], xa_w[:, 0, :], xa_s[:, 0, :], wa_w[:, cols], wa_s[:, cols])
            nc.scalar.copy(a_sb[0][:, cols], acc[:])

        def project_a(t):
            acc = psum.tile([P, H], F32, name="acc")
            product(acc[:], xa_w[:, t, :], xa_s[:, t, :], wa_w[:], wa_s[:])
            copy = nc.scalar.copy if False else nc.vector.tensor_copy
            copy(a_sb[t][:], acc[:])

        wb_w, wb_s = planes(N, "wb_q")
        z2_g = keep.tile([P, N, PACK], BF16, name="z2_g", align_bytes=64)
        z2_w, z2_s = planes(N, "z2_q")
        xb_w = pick(xw, two_l, U32, "xb_w", "wa_g1")

        def quantize_wb(h):
            cols = slice(h * HALF, (h + 1) * HALF)
            grouped = keep.tile([P, HALF, PACK], BF16, name="wb_g%d" % h, align_bytes=64)
            interleave(nc.vector.tensor_copy, grouped[:], wb_raw[h][:])
            quantize_into(wb_w[:, cols], wb_s[:, cols], grouped)

        def project_b(c):
            cols = slice(c * M, (c + 1) * M)
            bank = psum.tile([P, PACK, M], F32, name="acc")
            for t in range(PACK):
                product(bank[:, t, :], xb_w[:, t, :], xb_s[:, t, :], wb_w[:, cols], wb_s[:, cols])
            nc.vector.tensor_tensor(
                z2_g[:, cols, :],
                bank[:].rearrange("p t n -> p n t"),
                gi_sb[:].unsqueeze(1).to_broadcast([P, M, PACK]),
                ALU.mult,
            )
            if c == PACK - 1:
                quantize_into(z2_w[:], z2_s[:], z2_g)

        num = keep.tile([P, PACK, PACK, M], F32, name="num")
        den2 = keep.tile([P, PACK, PACK, M], F32, name="den2")

        def look(i):
            t, h = divmod(i, 2)
            cols = slice(h * HALF, (h + 1) * HALF)
            lcols = slice(h * HALF // 16, (h + 1) * HALF // 16)
            looked = ring.tile([P, 2, HALF], F32, name="looked", bufs=4)
            nc.scalar.activation(looked[:, 0, :], a_sb[t][:].indirect(n1_l[:, lcols]), ACT.Copy)
            nc.scalar.activation(looked[:, 1, :], a_sb[t][:].indirect(n2_l[:, lcols]), ACT.Copy)
            diff = ring.tile([P, 2, HALF], F32, name="diff")
            nc.vector.tensor_tensor(diff[:], looked[:], a_sb[t][:, cols].unsqueeze(1).to_broadcast([P, 2, HALF]), ALU.subtract)
            return looked, diff

        def weigh(i, looked, diff):
            t, h = divmod(i, 2)
            dealt = slice(h * HALF // PACK, (h + 1) * HALF // PACK)
            if i == 7:
                sq = keep.tile([P, 2, HALF], F32, name="sq_last", tag="handover")
            else:
                sq = ring.tile([P, 2, HALF], F32, name="sq")
            if False:
                nc.vector.tensor_tensor(sq[:], diff[:], diff[:], ALU.mult)
            else:
                nc.scalar.activation(sq[:], diff[:], ACT.Square)
            kern = ring.tile([P, 2, HALF], F32, name="kern")
            nc.scalar.activation(kern[:], sq[:], ACT.Exp, scale=-0.5)
            ksum = ring.tile([P, HALF], F32, name="ksum")
            den_out = den2[:, :, t, dealt].rearrange("p u m -> p m u")
            ksum_in = ksum[:].rearrange("p (m u) -> p m u", u=PACK)
            prod = ring.tile([P, 2, HALF], F32, name="prod")
            if i >= 6:
                nc.vector.scalar_tensor_tensor(ksum[:], kern[:, 0, :], 0.5, kern[:, 1, :], ALU.add, ALU.add)
                nc.vector.scalar_tensor_tensor(prod[:], kern[:], gt_sb[:, t : t + 1], looked[:], ALU.mult, ALU.mult)
                nc.vector.tensor_tensor(den_out, ksum_in, ksum_in, ALU.mult)
            else:
                nc.vector.tensor_tensor(ksum[:], kern[:, 0, :], kern[:, 1, :], ALU.add)
                nc.scalar.activation(den_out, ksum_in, ACT.Square, bias=half_c[:])
                nc.vector.scalar_tensor_tensor(prod[:], kern[:], gt_sb[:, t : t + 1], looked[:], ALU.mult, ALU.mult)
            nc.vector.tensor_tensor(
                num[:, :, t, dealt].rearrange("p u m -> p m u"),
                prod[:, 0, :].rearrange("p (m u) -> p m u", u=PACK),
                prod[:, 1, :].rearrange("p (m u) -> p m u", u=PACK),
                ALU.add,
            )

        side = [[(project_a, 2), (quantize_wb, 0)], [(project_a, 3), (quantize_wb, 1)], [(project_b, 0)], [(project_b, 1)], [(project_b, 2)], [(project_b, 3)], [], []]
        project_a(1)
        ahead = [look(i) for i in range(2)]
        for i in range(8):
            for step, arg in side[i]:
                step(arg)
            if i + 2 < 8:
                ahead.append(look(i + 2))
            weigh(i, *ahead[i])


        cv_sb = []
        for u in range(PACK):
            if u == 0:
                rec = keep.tile([P, PACK, M], F32, name="rec_first", tag="handover")
                nc.scalar.activation(rec[:, :3], den2[:, u, :3], ACT.Abs_reciprocal_sqrt)
                nc.scalar.activation(rec[:, 3], den2[:, u, 3], ACT.Abs_reciprocal_sqrt)
            else:
                rec = ring.tile([P, PACK, M], F32, name="rec")
                nc.scalar.activation(rec[:], den2[:, u], ACT.Abs_reciprocal_sqrt)
            z_g = keep.tile([P, M, PACK], BF16, name="z_g%d" % u, align_bytes=64)
            for m0 in (0, M // 2):
                ms = slice(m0, m0 + M // 2)
                nc.vector.tensor_tensor(
                    z_g[:, ms, :].rearrange("p (c i) t -> p c t i", i=4),
                    num[:, u, :, ms].rearrange("p t (c i) -> p c t i", i=4),
                    rec[:, :, ms].rearrange("p t (c i) -> p c t i", i=4),
                    ALU.mult,
                )
            z_w, z_s = quantize(z_g, M, "z_q%d" % u)
            acc = psum.tile([P, N], F32, name="acc")
            nc.tensor.matmul_mx(
                out=acc[:],
                lhsT=z_w[:].bitcast(FP8X4),
                lhsT_scale=z_s[:],
                rhs=z2_w[:].bitcast(FP8X4),
                rhs_scale=z2_s[:],
                start=True,
                stop=True,
            )
            cv_u = keep.tile([P, N], F32, name="cv%d" % u)
            if u < 2:
                nc.scalar.activation(cv_u[:], acc[:], ACT.Copy, scale=0.0625)
            else:
                nc.vector.tensor_scalar(cv_u[:], acc[:], 0.0625, None, ALU.mult)
            cv_sb.append(cv_u)

        y_w = keep.tile([P, N], U32, name="y_w", align_bytes=64)
        y_s = keep.tile([P, N], U8, name="y_s", align_bytes=64)
        rows = out_0.rearrange("(p u) c -> p u c", u=PACK)
        words = out_1[0].rearrange("p c t -> p (c t)").bitcast(I32)
        for h, (c0, width) in enumerate(((0, 256), (256, 128), (384, 128))):
            cols = slice(c0, c0 + width)
            lcols = slice(c0 // 16, (c0 + width) // 16)
            y = keep.tile([P, PACK, width], F32, name="y%d" % h)
            for u in range(PACK):
                other = ring.tile([P, width], F32, name="other", bufs=4)
                nc.scalar.activation(other[:], cv_sb[u][:].indirect(n3_l[:, lcols]), ACT.Copy)
                nc.vector.tensor_tensor(y[:, u, :], cv_sb[u][:, cols], other[:], ALU.max)
            nc.sync.dma_start(rows[:, :, cols], y[:])
            y_g = keep.tile([P, width, PACK], BF16, name="y_g%d" % h, align_bytes=64)
            interleave(nc.vector.tensor_copy, y_g[:], y[:])
            nc.vector.quantize_mx(out=y_w[:, cols].bitcast(FP8X4), scales=y_s[:, cols], in_=y_g[:].rearrange("p c t -> p (c t)"))
            nc.sync.dma_start(words[:, cols], y_w[:, cols].bitcast(I32))
        for q in range(4):
            queue = nc.sync if q % 2 == 0 else nc.scalar
            queue.dma_start(out_2[0, 4 * q : 4 * q + 4, :].bitcast(I32), y_s[32 * q : 32 * q + 4, :].bitcast(I32))
